import numpy as np
import ml_dtypes


def mxq(x, axis, fmt="e4m3"):
    dtype, down = {"e4m3": (ml_dtypes.float8_e4m3fn, 7), "e5m2": (ml_dtypes.float8_e5m2, 14)}[fmt]
    v = np.moveaxis(np.asarray(x, np.float32).astype(ml_dtypes.bfloat16).astype(np.float64), axis, -1)
    blocks = v.reshape(v.shape[:-1] + (-1, 32))
    amax = np.abs(blocks).max(-1, keepdims=True)
    byte = np.maximum(np.where(amax > 0, np.frexp(amax)[1] - 1 + 127, 0) - down, 1)
    scale = np.exp2(byte - 127.0)
    codes = (blocks / scale).astype(np.float32).astype(dtype).astype(np.float64)
    return np.moveaxis((codes * scale).reshape(v.shape), -1, axis)


WIDE = False


def mx_kscale(k):
    if not WIDE:
        return np.ones(k)
    levels = np.array([10, -10, 5, -5, 0])
    if k % 512:
        return np.exp2(np.random.permutation(np.resize(levels, k // 32))).repeat(32)
    a = np.empty((k // 512, 16))
    for p in range(k // 512):
        a[p, :8] = np.random.permutation(np.resize(levels, 8))
        for g in range(8):
            far = levels[np.abs(levels - a[p, g]) >= 10]
            a[p, g + 8] = far[np.random.randint(len(far))]
    return np.exp2(a.ravel()).repeat(32)


def f64(x):
    return np.asarray(x).astype(np.float64)


def striped(idx):
    return np.tile(np.asarray(idx).reshape(-1, 16).T, (8, 1)).astype(np.uint16)


def unstriped(offs):
    return offs[:16].T.reshape(-1).astype(np.int64)


E2M1 = np.array([0.0, 0.5, 1.0, 1.5, 2.0, 3.0, 4.0, 6.0, -0.0, -0.5, -1.0, -1.5, -2.0, -3.0, -4.0, -6.0])


def pack_weight(w, fmt):
    k, n = w.shape
    w = f64(np.asarray(w, np.float32).astype(ml_dtypes.bfloat16)).reshape(k // 32, 32, n)
    amax = np.abs(w).max(1)
    if fmt == "e4m3":
        byte = np.frexp(amax)[1] - 1 + 127 - 7
    else:
        mant, ex = np.frexp(amax / 6.0)
        byte = np.where(mant > 0.5, ex, ex - 1) + 127
    byte = np.clip(np.where(amax > 0, byte, 1), 1, 254)
    scaled = (w * np.exp2(127.0 - byte)[:, None, :]).reshape(k, n).astype(np.float32)
    by_word = np.ascontiguousarray(scaled.reshape(k // 512, 128, 4, n).transpose(0, 1, 3, 2))
    if fmt == "e4m3":
        words = by_word.astype(ml_dtypes.float8_e4m3fn).view(np.uint8)
    else:
        c = by_word.astype(ml_dtypes.float4_e2m1fn).view(np.uint8) & 0xF
        words = (c[..., 0::2] | (c[..., 1::2] << 4)).reshape(k // 512, 128, 2 * n)
    return np.ascontiguousarray(words), np.ascontiguousarray(byte.astype(np.uint8).reshape(k // 512, 16, n))


def unpack_weight(words, scales, fmt):
    g, _, n = scales.shape
    words = np.ascontiguousarray(words).reshape(g, 128, n, -1)
    if fmt == "e4m3":
        vals = words.view(ml_dtypes.float8_e4m3fn).astype(np.float64)
    else:
        nib = np.empty((g, 128, n, 4), np.uint8)
        nib[..., 0::2] = words & 0xF
        nib[..., 1::2] = words >> 4
        vals = E2M1[nib]
    vals = vals * np.repeat(np.exp2(scales.astype(np.float64) - 127.0), 8, axis=1)[..., None]
    return vals.transpose(0, 1, 3, 2).reshape(g * 512, n)


def bf(x):
    return np.asarray(x, np.float32).astype(ml_dtypes.bfloat16)


def planes(Y):
    r, m = Y.shape
    b = f64(bf(Y)).reshape(r // 32, 32, m)
    amax = np.abs(b).max(1)
    byte = np.clip(np.where(amax > 0, np.frexp(amax)[1] - 1 + 127 - 7, 1), 1, 254)
    codes = (b * np.exp2(127.0 - byte)[:, None, :]).reshape(r, m).astype(np.float32).astype(ml_dtypes.float8_e4m3fn).view(np.uint8)
    words = codes.reshape(r // 512, 128, 4, m).transpose(0, 1, 3, 2)
    return np.ascontiguousarray(words), np.ascontiguousarray(byte.astype(np.uint8).reshape(r // 512, 16, m))


D, T, I, Q, E, Z, M = 512, 2048, 512, 256, 512, 1024, 1024


def setup_inputs():
    n = np.random.standard_normal
    idx = np.random.permutation(T)[:I]
    idx2 = np.random.permutation(Z)[:I]
    idx3 = np.random.permutation(Z)[:I]
    idx4 = np.random.permutation(M)[:Q]
    fd = mx_kscale(D)
    fi = mx_kscale(I)
    ti = np.ones(T)
    ti[idx] = fi
    keysp = pack_weight(n((D, T)) / fd[:, None], "e2m1")
    return {
        "query": (n((D, Q)) * 1.0 / np.sqrt(D) * fd[:, None]).astype(np.float32),
        "keys_words": keysp[0],
        "keys_scales": keysp[1],
        "os": (np.random.uniform(0.02, 0.08, (1, I)) * fi).astype(np.float32),
        "vals": (n((E, T)) / ti).astype(np.float32),
        "member": (n((E, M))).astype(np.float32),
        "mgain": np.tile(np.random.uniform(0.5, 2.0, M), (128, 1)).astype(np.float32),
        "offs": striped(idx),
        "offs2": striped(idx2),
        "offs3": striped(idx3),
        "offs4": striped(idx4),
    }


def reference(query, keys_words, keys_scales, os, vals, member, mgain, offs, offs2, offs3, offs4):
    idx = unstriped(offs)
    idx2 = unstriped(offs2)
    idx3 = unstriped(offs3)
    idx4 = unstriped(offs4)
    keysu = unpack_weight(keys_words, keys_scales, "e2m1")
    queryq = mxq(f64(query), 0, "e4m3")
    keysidxg = keysu[:, idx]
    a = queryq.T @ keysidxg
    f0 = np.zeros((Q, Z))
    f0[:, idx2] = a
    s = a + f0[:, idx3]
    w = np.maximum(s, 0.0)
    wo1 = w * f64(os)
    wt1 = wo1.T
    vt1 = f64(vals)[:, idx].T
    vt1q = mxq(vt1, 0, "e4m3")
    wt1q = mxq(wt1, 0, "e4m3")
    o = vt1q.T @ wt1q
    y = o * f64(mgain)[:1][:, idx4] + f64(member)[:, idx4]
    words, scales = planes(y)
    return y, words, scales

@@ -1,0 +1,214 @@
+from contextlib import ExitStack
+
+import concourse.mybir as mybir
+from concourse.masks import make_identity
+
+D, T, I, Q, E, Z, M = 512, 2048, 512, 256, 512, 1024, 1024
+FLOPS = 2 * D * Q * I + 2 * I * E * Q
+BYTES = 4 * (D * Q + I + E * T + E * M + M + E * Q) + D * T // 2 + D * T // 32 + 256 * (3 * I + Q) // 16 + E * Q + E * Q // 32
+
+F32 = mybir.dt.float32
+BF16 = mybir.dt.bfloat16
+I32 = mybir.dt.int32
+U32 = mybir.dt.uint32
+U16 = mybir.dt.uint16
+U8 = mybir.dt.uint8
+FP8X4 = mybir.dt.float8_e4m3fn_x4
+FP4X4 = mybir.dt.float4_e2m1fn_x4
+ALU = mybir.AluOpType
+COPY = mybir.ActivationFunctionType.Copy
+
+P = 128
+PACK = 4
+Q_TILES = Q // P
+HALF = I // 2
+
+
+def tile_attend_passedthrough_bymember_lean_pl_kernel(
+    tc, query, keys_words, keys_scales, slot_factor, vals, member, mgain, offs, offs2, offs3, offs4, out_0, out_1, out_2
+):
+    nc = tc.nc
+    with ExitStack() as ctx:
+        sb = ctx.enter_context(tc.tile_pool(name="sb", bufs=1))
+        ps = ctx.enter_context(tc.psum_pool(name="ps", bufs=1))
+
+        kscale_pool = sb.tile([P, T], U8, align_bytes=64)
+        nc.gpsimd.memset(kscale_pool[:].bitcast(I32), 0)
+        gain_pool = sb.tile([P, M], F32)
+        nc.vector.memset(gain_pool[:], 0.0)
+        f0 = [sb.tile([P, Z], F32, name=f"f0_{h}", tag=f"f0_{h}", align_bytes=64) for h in range(Q_TILES)]
+        for h in range(Q_TILES):
+            nc.vector.memset(f0[h][:], 0.0)
+        ident = sb.tile([P, P], F32)
+        make_identity(nc, ident[:])
+
+        for g in range(4):
+            nc.sync.dma_start(
+                kscale_pool[32 * g : 32 * g + 4, :].bitcast(I32), keys_scales[0, 4 * g : 4 * g + 4, :].bitcast(I32)
+            )
+        idx = sb.tile([P, I // 16], U16)
+        nc.sync.dma_start(idx[:], offs)
+        idx2 = sb.tile([P, I // 16], U16)
+        nc.sync.dma_start(idx2[:], offs2)
+        kword_pool = sb.tile([P, T], U16, align_bytes=64)
+        nc.sync.dma_start(kword_pool[:].bitcast(I32), keys_words[0].bitcast(I32))
+        q_raw = sb.tile([P, PACK, Q], F32)
+        nc.sync.dma_start(q_raw[:], query.rearrange("(p t) q -> p t q", t=PACK))
+        idx4 = sb.tile([P, Q // 16], U16)
+        nc.sync.dma_start(idx4[:], offs4)
+        nc.sync.dma_start(gain_pool[0:1, :], mgain[0:1, :])
+        vals_planes = vals.rearrange("(p j) t -> j p t", j=PACK)
+        member_planes = member.rearrange("(p j) m -> j p m", j=PACK)
+        val_pool = [
+            sb.tile([P, T], F32, name=f"val_pool{j}", tag=f"val_pool{j}", align_bytes=64) for j in range(PACK)
+        ]
+        member_pool = [
+            sb.tile([P, M], F32, name=f"member_pool{j}", tag=f"member_pool{j}", align_bytes=64) for j in range(PACK)
+        ]
+        nc.sync.dma_start(val_pool[0][:], vals_planes[0])
+        idx3 = sb.tile([P, I // 16], U16)
+        nc.sync.dma_start(idx3[:], offs3)
+        os4 = sb.tile([P, PACK], F32)
+        nc.sync.dma_start(os4[:], slot_factor.rearrange("o (p t) -> p (o t)", t=PACK))
+        for j in range(1, PACK):
+            nc.sync.dma_start(val_pool[j][:], vals_planes[j])
+        for j in range(PACK):
+            nc.sync.dma_start(member_pool[j][:], member_planes[j])
+
+        slots = [slice(half * HALF, (half + 1) * HALF) for half in range(2)]
+        entries = [slice(half * HALF // 16, (half + 1) * HALF // 16) for half in range(2)]
+        k_words = [sb.tile([P, HALF], U16, align_bytes=64, name=f"k_words{half}") for half in range(2)]
+        k_scales = [sb.tile([P, HALF], U8, align_bytes=64, name=f"k_scales{half}") for half in range(2)]
+        for half in range(2):
+            nc.vector.tensor_copy(k_words[half][:], kword_pool[:].indirect(idx[:, entries[half]]))
+        nc.vector.tensor_copy(k_scales[0][:], kscale_pool[:].indirect(idx[:, entries[0]]))
+        q_codes = [sb.tile([P, P], U32, align_bytes=64, name=f"q_codes{h}") for h in range(Q_TILES)]
+        q_scales = [sb.tile([P, P], U8, align_bytes=64, name=f"q_scales{h}") for h in range(Q_TILES)]
+        for h in range(Q_TILES):
+            q_bf = sb.tile([P, P, PACK], BF16, align_bytes=64, name=f"q_bf{h}")
+            nc.scalar.activation(
+                q_bf[:].rearrange("p (c i) t -> p c t i", i=4),
+                q_raw[:, :, h * P : (h + 1) * P].rearrange("p t (c i) -> p c t i", i=4),
+                COPY,
+            )
+            nc.vector.quantize_mx(
+                q_codes[h][:].bitcast(FP8X4), q_scales[h][:], q_bf[:].rearrange("p q t -> p (q t)")
+            )
+        nc.vector.tensor_copy(k_scales[1][:], kscale_pool[:].indirect(idx[:, entries[1]]))
+
+        a_sb = [sb.tile([P, I], F32, name=f"a_sb{h}") for h in range(Q_TILES)]
+        for half in range(2):
+            for h in range(Q_TILES):
+                a_ps = ps.tile([P, HALF], F32, tag=f"bank{2 * half + h}")
+                nc.tensor.matmul_mx(
+                    a_ps[:], q_codes[h][:].bitcast(FP8X4), q_scales[h][:], k_words[half][:].bitcast(FP4X4),
+                    k_scales[half][:], start=True, stop=True,
+                )
+                nc.scalar.copy(a_sb[h][:, slots[half]], a_ps[:])
+        for half in range(2):
+            nc.vector.tensor_copy(f0[0][:].indirect(idx2[:, entries[half]]), a_sb[0][:, slots[half]])
+            nc.scalar.activation(f0[1][:].indirect(idx2[:, entries[half]]), a_sb[1][:, slots[half]], COPY)
+
+        passed = [sb.tile([P, I], F32, name=f"passed{h}") for h in range(Q_TILES)]
+        nc.vector.tensor_copy(passed[0][:], f0[0][:].indirect(idx3[:]))
+        nc.scalar.activation(passed[1][:], f0[1][:].indirect(idx3[:]), COPY)
+        st_ps = [ps.tile([P, PACK, P], F32, tag=f"bank{h}", name=f"st_ps{h}") for h in range(Q_TILES)]
+        for h in range(Q_TILES):
+            for t in range(PACK):
+                nc.tensor.matmul(
+                    st_ps[h][:, t, :], a_sb[h][:, t::PACK], ident[:], start=(t == 0), stop=False, is_transpose=True
+                )
+        w_bf = sb.tile([P, Q, PACK], BF16, align_bytes=64)
+        w_codes = sb.tile([P, Q], U32, align_bytes=64)
+        w_scales = sb.tile([P, Q], U8, align_bytes=64)
+        for h in range(Q_TILES):
+            for t in range(PACK):
+                nc.tensor.matmul(
+                    st_ps[h][:, t, :], passed[h][:, t::PACK], ident[:], start=False, stop=(t == PACK - 1),
+                    is_transpose=True,
+                )
+            nc.vector.scalar_tensor_tensor(
+                w_bf[:, h * P : (h + 1) * P, :],
+                st_ps[h][:].rearrange("p t q -> p q t"),
+                0.0,
+                os4[:].unsqueeze(1).to_broadcast([P, P, PACK]),
+                ALU.max,
+                ALU.mult,
+            )
+        nc.vector.quantize_mx(w_codes[:].bitcast(FP8X4), w_scales[:], w_bf[:].rearrange("p q t -> p (q t)"))
+
+        gain_row = sb.tile([P, Q], F32)
+        nc.scalar.activation(gain_row[:], gain_pool[:].indirect(idx4[:]), COPY)
+        gain_ps = ps.tile([P, Q_TILES, P], F32, tag="bank4")
+        for h in range(Q_TILES):
+            nc.tensor.transpose(gain_ps[:, h, :], gain_row[:, h * P : (h + 1) * P], ident[:])
+        gain_col = sb.tile([P, Q_TILES], F32)
+        nc.scalar.copy(gain_col[:], gain_ps[:, :, 0])
+        gain_ps2 = ps.tile([P, Q_TILES, P], F32, tag="bank5")
+        for h in range(Q_TILES):
+            nc.tensor.transpose(gain_ps2[:, h, :], gain_col[:, h : h + 1].to_broadcast([P, P]), ident[:])
+        gain = sb.tile([P, Q], F32)
+        nc.scalar.copy(gain[:], gain_ps2[:].rearrange("p h q -> p (h q)"))
+
+        v_listed = [
+            sb.tile([P, I], BF16, name=f"v_listed{j}", tag=f"f0_{j}" if j < 2 else f"v_listed{j}", align_bytes=64)
+            for j in range(PACK)
+        ]
+        for j in range(PACK):
+            if j in (0, 3):
+                nc.vector.tensor_copy(v_listed[j][:], val_pool[j][:].indirect(idx[:]))
+            else:
+                nc.scalar.activation(v_listed[j][:], val_pool[j][:].indirect(idx[:]), COPY)
+        m_listed = [sb.tile([P, Q], F32, name=f"m_listed{j}") for j in range(PACK)]
+        for j in range(PACK):
+            nc.scalar.activation(m_listed[j][:], member_pool[j][:].indirect(idx4[:]), COPY)
+        og = sb.tile([P, PACK, Q], F32)
+        for pair in range(2):
+            vt_ps = ps.tile([P, 2, 2, P], F32, tag=f"bank{pair}")
+            for c in range(2):
+                words = v_listed[2 * pair + c][:].bitcast(F32)
+                for u in range(2):
+                    nc.tensor.transpose(vt_ps[:, c, u, :], words[:, u::2], ident[:])
+            v_bf = sb.tile(
+                [P, 2 * P * PACK], BF16, align_bytes=64, name=f"v_bf{pair}", tag=("val_pool2", "member_pool0")[pair]
+            )
+            nc.scalar.copy(
+                v_bf[:].bitcast(F32).rearrange("p (c e u) -> p c e u", c=2, u=2),
+                vt_ps[:].rearrange("p c u e -> p c e u"),
+            )
+            v_codes = sb.tile(
+                [P, 2 * P], U32, align_bytes=64, name=f"v_codes{pair}", tag=("val_pool3", "v_codes1")[pair]
+            )
+            v_scales = sb.tile([P, 2 * P], U8, align_bytes=64, name=f"v_scales{pair}")
+            nc.vector.quantize_mx(v_codes[:].bitcast(FP8X4), v_scales[:], v_bf[:])
+            o_ps = ps.tile([P, 2, Q], F32, tag=f"bank{2 + pair}")
+            for c in range(2):
+                cols = slice(c * P, (c + 1) * P)
+                nc.tensor.matmul_mx(
+                    o_ps[:, c, :], v_codes[:, cols].bitcast(FP8X4), v_scales[:, cols], w_codes[:].bitcast(FP8X4),
+                    w_scales[:], start=True, stop=True,
+                )
+            nc.vector.tensor_tensor(
+                og[:, 2 * pair : 2 * pair + 2, :], o_ps[:], gain[:].unsqueeze(1).to_broadcast([P, 2, Q]), ALU.mult
+            )
+
+        y = sb.tile([P, PACK, Q], F32)
+        for j in range(PACK):
+            nc.vector.tensor_tensor(y[:, j, :], m_listed[j][:], og[:, j, :], ALU.add)
+        y_rows = out_0.rearrange("(p t) q -> p t q", t=PACK)
+        nc.sync.dma_start(y_rows[:, : PACK - 1, :], y[:, : PACK - 1, :])
+        nc.sync.dma_start(y_rows[:, PACK - 1, :], y[:, PACK - 1, :])
+
+        y_bf = sb.tile([P, Q, PACK], BF16, align_bytes=64)
+        nc.vector.tensor_copy(
+            y_bf[:].rearrange("p (c i) t -> p c t i", i=4), y[:].rearrange("p t (c i) -> p c t i", i=4)
+        )
+        y_codes = sb.tile([P, Q], U32, align_bytes=64)
+        y_scales = sb.tile([P, Q], U8, align_bytes=64)
+        nc.vector.quantize_mx(y_codes[:].bitcast(FP8X4), y_scales[:], y_bf[:].rearrange("p q t -> p (q t)"))
+        nc.sync.dma_start(out_1[0].rearrange("p c r -> p (c r)").bitcast(I32), y_codes[:].bitcast(I32))
+        for g in range(4):
+            queue = nc.sync if g % 2 == 0 else nc.scalar
+            queue.dma_start(
+                out_2[0, 4 * g : 4 * g + 4, :].bitcast(I32), y_scales[32 * g : 32 * g + 4, :].bitcast(I32)
+            )

@@ -34,29 +34,29 @@ def tile_attend_passedthrough_bymember_lean_pl_kernel(
 
         kscale_pool = sb.tile([P, T], U8, align_bytes=64)
         nc.gpsimd.memset(kscale_pool[:].bitcast(I32), 0)
-        gain_pool = sb.tile([P, M], F32)
-        nc.vector.memset(gain_pool[:], 0.0)
+        ident = sb.tile([P, P], F32)
+        nc.vector.memset(ident[:], 0.0)
+        make_identity(nc, ident[:], nomemset=True)
         f0 = [sb.tile([P, Z], F32, name=f"f0_{h}", tag=f"f0_{h}", align_bytes=64) for h in range(Q_TILES)]
         for h in range(Q_TILES):
             nc.vector.memset(f0[h][:], 0.0)
-        ident = sb.tile([P, P], F32)
-        make_identity(nc, ident[:])
 
-        for g in range(4):
-            nc.sync.dma_start(
-                kscale_pool[32 * g : 32 * g + 4, :].bitcast(I32), keys_scales[0, 4 * g : 4 * g + 4, :].bitcast(I32)
-            )
-        idx = sb.tile([P, I // 16], U16)
-        nc.sync.dma_start(idx[:], offs)
-        idx2 = sb.tile([P, I // 16], U16)
-        nc.sync.dma_start(idx2[:], offs2)
+        gain_rows = sb.tile([P, M // P], F32, tag="q_bf", align_bytes=64)
+        nc.scalar.dma_start(gain_rows[:], mgain[0:1, :].rearrange("o (p j) -> p (o j)", p=P))
         kword_pool = sb.tile([P, T], U16, align_bytes=64)
         nc.sync.dma_start(kword_pool[:].bitcast(I32), keys_words[0].bitcast(I32))
-        q_raw = sb.tile([P, PACK, Q], F32)
+        idx = sb.tile([P, I // 16], U16)
+        nc.sync.dma_start(idx[:], offs)
+        q_raw = sb.tile([P, PACK, Q], F32, tag="q_raw")
         nc.sync.dma_start(q_raw[:], query.rearrange("(p t) q -> p t q", t=PACK))
+        for g in range(4):
+            nc.scalar.dma_start(
+                kscale_pool[32 * g : 32 * g + 4, :].bitcast(I32), keys_scales[0, 4 * g : 4 * g + 4, :].bitcast(I32)
+            )
         idx4 = sb.tile([P, Q // 16], U16)
         nc.sync.dma_start(idx4[:], offs4)
-        nc.sync.dma_start(gain_pool[0:1, :], mgain[0:1, :])
+        idx2 = sb.tile([P, I // 16], U16)
+        nc.sync.dma_start(idx2[:], offs2)
         vals_planes = vals.rearrange("(p j) t -> j p t", j=PACK)
         member_planes = member.rearrange("(p j) m -> j p m", j=PACK)
         val_pool = [
@@ -75,26 +75,40 @@ def tile_attend_passedthrough_bymember_lean_pl_kernel(
         for j in range(PACK):
             nc.sync.dma_start(member_pool[j][:], member_planes[j])
 
+        gain_pool = sb.tile([P, M], F32, tag="gain_pool", align_bytes=64)
+        for half in range(2):
+            gain_ps = ps.tile([P, 4, P], F32, tag=f"bank{4 + half}")
+            for c in range(4):
+                j = 4 * half + c
+                nc.tensor.transpose(gain_ps[:, c, :], gain_rows[:, j : j + 1].to_broadcast([P, P]), ident[:])
+            nc.scalar.activation(
+                gain_pool[:].rearrange("p (r j) -> p r j", j=M // P)[:, :, 4 * half : 4 * half + 4],
+                gain_ps[:].rearrange("p c r -> p r c"),
+                COPY,
+            )
+
         slots = [slice(half * HALF, (half + 1) * HALF) for half in range(2)]
         entries = [slice(half * HALF // 16, (half + 1) * HALF // 16) for half in range(2)]
         k_words = [sb.tile([P, HALF], U16, align_bytes=64, name=f"k_words{half}") for half in range(2)]
         k_scales = [sb.tile([P, HALF], U8, align_bytes=64, name=f"k_scales{half}") for half in range(2)]
         for half in range(2):
             nc.vector.tensor_copy(k_words[half][:], kword_pool[:].indirect(idx[:, entries[half]]))
-        nc.vector.tensor_copy(k_scales[0][:], kscale_pool[:].indirect(idx[:, entries[0]]))
+        for half in range(2):
+            nc.vector.tensor_copy(k_scales[half][:], kscale_pool[:].indirect(idx[:, entries[half]]))
         q_codes = [sb.tile([P, P], U32, align_bytes=64, name=f"q_codes{h}") for h in range(Q_TILES)]
         q_scales = [sb.tile([P, P], U8, align_bytes=64, name=f"q_scales{h}") for h in range(Q_TILES)]
+        q_bf = sb.tile([P, Q * PACK], BF16, align_bytes=64, tag="q_bf")
         for h in range(Q_TILES):
-            q_bf = sb.tile([P, P, PACK], BF16, align_bytes=64, name=f"q_bf{h}")
+            q_tile = q_bf[:, h * P * PACK : (h + 1) * P * PACK]
             nc.scalar.activation(
-                q_bf[:].rearrange("p (c i) t -> p c t i", i=4),
+                q_tile.rearrange("p (c i t) -> p c t i", i=4, t=PACK),
                 q_raw[:, :, h * P : (h + 1) * P].rearrange("p t (c i) -> p c t i", i=4),
                 COPY,
             )
-            nc.vector.quantize_mx(
-                q_codes[h][:].bitcast(FP8X4), q_scales[h][:], q_bf[:].rearrange("p q t -> p (q t)")
-            )
-        nc.vector.tensor_copy(k_scales[1][:], kscale_pool[:].indirect(idx[:, entries[1]]))
+            nc.vector.quantize_mx(q_codes[h][:].bitcast(FP8X4), q_scales[h][:], q_tile)
+
+        gain = sb.tile([P, Q], F32, tag="q_raw")
+        nc.vector.tensor_copy(gain[:], gain_pool[:].indirect(idx4[:]))
 
         a_sb = [sb.tile([P, I], F32, name=f"a_sb{h}") for h in range(Q_TILES)]
         for half in range(2):
@@ -104,12 +118,15 @@ def tile_attend_passedthrough_bymember_lean_pl_kernel(
                     a_ps[:], q_codes[h][:].bitcast(FP8X4), q_scales[h][:], k_words[half][:].bitcast(FP4X4),
                     k_scales[half][:], start=True, stop=True,
                 )
-                nc.scalar.copy(a_sb[h][:, slots[half]], a_ps[:])
+                if h == 0:
+                    nc.vector.tensor_copy(a_sb[h][:, slots[half]], a_ps[:])
+                else:
+                    nc.scalar.copy(a_sb[h][:, slots[half]], a_ps[:])
         for half in range(2):
             nc.vector.tensor_copy(f0[0][:].indirect(idx2[:, entries[half]]), a_sb[0][:, slots[half]])
             nc.scalar.activation(f0[1][:].indirect(idx2[:, entries[half]]), a_sb[1][:, slots[half]], COPY)
 
-        passed = [sb.tile([P, I], F32, name=f"passed{h}") for h in range(Q_TILES)]
+        passed = [sb.tile([P, I], F32, name=f"passed{h}", tag=f"passed{h}", align_bytes=64) for h in range(Q_TILES)]
         nc.vector.tensor_copy(passed[0][:], f0[0][:].indirect(idx3[:]))
         nc.scalar.activation(passed[1][:], f0[1][:].indirect(idx3[:]), COPY)
         st_ps = [ps.tile([P, PACK, P], F32, tag=f"bank{h}", name=f"st_ps{h}") for h in range(Q_TILES)]
@@ -118,7 +135,7 @@ def tile_attend_passedthrough_bymember_lean_pl_kernel(
                 nc.tensor.matmul(
                     st_ps[h][:, t, :], a_sb[h][:, t::PACK], ident[:], start=(t == 0), stop=False, is_transpose=True
                 )
-        w_bf = sb.tile([P, Q, PACK], BF16, align_bytes=64)
+        w_bf = sb.tile([P, Q, PACK], BF16, align_bytes=64, tag="w_bf")
         w_codes = sb.tile([P, Q], U32, align_bytes=64)
         w_scales = sb.tile([P, Q], U8, align_bytes=64)
         for h in range(Q_TILES):
@@ -137,21 +154,8 @@ def tile_attend_passedthrough_bymember_lean_pl_kernel(
             )
         nc.vector.quantize_mx(w_codes[:].bitcast(FP8X4), w_scales[:], w_bf[:].rearrange("p q t -> p (q t)"))
 
-        gain_row = sb.tile([P, Q], F32)
-        nc.scalar.activation(gain_row[:], gain_pool[:].indirect(idx4[:]), COPY)
-        gain_ps = ps.tile([P, Q_TILES, P], F32, tag="bank4")
-        for h in range(Q_TILES):
-            nc.tensor.transpose(gain_ps[:, h, :], gain_row[:, h * P : (h + 1) * P], ident[:])
-        gain_col = sb.tile([P, Q_TILES], F32)
-        nc.scalar.copy(gain_col[:], gain_ps[:, :, 0])
-        gain_ps2 = ps.tile([P, Q_TILES, P], F32, tag="bank5")
-        for h in range(Q_TILES):
-            nc.tensor.transpose(gain_ps2[:, h, :], gain_col[:, h : h + 1].to_broadcast([P, P]), ident[:])
-        gain = sb.tile([P, Q], F32)
-        nc.scalar.copy(gain[:], gain_ps2[:].rearrange("p h q -> p (h q)"))
-
         v_listed = [
-            sb.tile([P, I], BF16, name=f"v_listed{j}", tag=f"f0_{j}" if j < 2 else f"v_listed{j}", align_bytes=64)
+            sb.tile([P, I], BF16, name=f"v_listed{j}", tag=("f0_0", "f0_1", "passed1", "passed0")[j], align_bytes=64)
             for j in range(PACK)
         ]
         for j in range(PACK):
@@ -159,18 +163,22 @@ def tile_attend_passedthrough_bymember_lean_pl_kernel(
                 nc.vector.tensor_copy(v_listed[j][:], val_pool[j][:].indirect(idx[:]))
             else:
                 nc.scalar.activation(v_listed[j][:], val_pool[j][:].indirect(idx[:]), COPY)
-        m_listed = [sb.tile([P, Q], F32, name=f"m_listed{j}") for j in range(PACK)]
-        for j in range(PACK):
+        m_tags = ("passed0", "m1", "m2", "m3")
+        m_listed = [None] * PACK
+
+        def gather_member(j):
+            m_listed[j] = sb.tile([P, Q], F32, name=f"m_listed{j}", tag=m_tags[j], align_bytes=64)
             nc.scalar.activation(m_listed[j][:], member_pool[j][:].indirect(idx4[:]), COPY)
+
         og = sb.tile([P, PACK, Q], F32)
         for pair in range(2):
-            vt_ps = ps.tile([P, 2, 2, P], F32, tag=f"bank{pair}")
+            vt_ps = ps.tile([P, 2, 2, P], F32, tag=f"bank{4 * pair}")
             for c in range(2):
                 words = v_listed[2 * pair + c][:].bitcast(F32)
                 for u in range(2):
                     nc.tensor.transpose(vt_ps[:, c, u, :], words[:, u::2], ident[:])
             v_bf = sb.tile(
-                [P, 2 * P * PACK], BF16, align_bytes=64, name=f"v_bf{pair}", tag=("val_pool2", "member_pool0")[pair]
+                [P, 2 * P * PACK], BF16, align_bytes=64, name=f"v_bf{pair}", tag=("val_pool2", "v_bf1")[pair]
             )
             nc.scalar.copy(
                 v_bf[:].bitcast(F32).rearrange("p (c e u) -> p c e u", c=2, u=2),
@@ -193,6 +201,8 @@ def tile_attend_passedthrough_bymember_lean_pl_kernel(
             )
 
         y = sb.tile([P, PACK, Q], F32)
+        for j in range(PACK):
+            gather_member(j)
         for j in range(PACK):
             nc.vector.tensor_tensor(y[:, j, :], m_listed[j][:], og[:, j, :], ALU.add)
         y_rows = out_0.rearrange("(p t) q -> p t q", t=PACK)

@@ -47,7 +47,7 @@ def tile_attend_passedthrough_bymember_lean_pl_kernel(
         nc.sync.dma_start(kword_pool[:].bitcast(I32), keys_words[0].bitcast(I32))
         idx = sb.tile([P, I // 16], U16)
         nc.sync.dma_start(idx[:], offs)
-        q_raw = sb.tile([P, PACK, Q], F32, tag="q_raw")
+        q_raw = sb.tile([P, PACK, Q], F32, tag="q_raw", align_bytes=64)
         nc.sync.dma_start(q_raw[:], query.rearrange("(p t) q -> p t q", t=PACK))
         for g in range(4):
             nc.scalar.dma_start(
@@ -90,11 +90,10 @@ def tile_attend_passedthrough_bymember_lean_pl_kernel(
         slots = [slice(half * HALF, (half + 1) * HALF) for half in range(2)]
         entries = [slice(half * HALF // 16, (half + 1) * HALF // 16) for half in range(2)]
         k_words = [sb.tile([P, HALF], U16, align_bytes=64, name=f"k_words{half}") for half in range(2)]
-        k_scales = [sb.tile([P, HALF], U8, align_bytes=64, name=f"k_scales{half}") for half in range(2)]
         for half in range(2):
             nc.vector.tensor_copy(k_words[half][:], kword_pool[:].indirect(idx[:, entries[half]]))
-        for half in range(2):
-            nc.vector.tensor_copy(k_scales[half][:], kscale_pool[:].indirect(idx[:, entries[half]]))
+        k_scales = [sb.tile([P, HALF], U8, align_bytes=64, name="k_scales0")]
+        nc.vector.tensor_copy(k_scales[0][:], kscale_pool[:].indirect(idx[:, entries[0]]))
         q_codes = [sb.tile([P, P], U32, align_bytes=64, name=f"q_codes{h}") for h in range(Q_TILES)]
         q_scales = [sb.tile([P, P], U8, align_bytes=64, name=f"q_scales{h}") for h in range(Q_TILES)]
         q_bf = sb.tile([P, Q * PACK], BF16, align_bytes=64, tag="q_bf")
@@ -107,8 +106,10 @@ def tile_attend_passedthrough_bymember_lean_pl_kernel(
             )
             nc.vector.quantize_mx(q_codes[h][:].bitcast(FP8X4), q_scales[h][:], q_tile)
 
-        gain = sb.tile([P, Q], F32, tag="q_raw")
-        nc.vector.tensor_copy(gain[:], gain_pool[:].indirect(idx4[:]))
+        k_scales.append(sb.tile([P, HALF], U8, align_bytes=64, name="k_scales1", tag="q_raw"))
+        nc.vector.tensor_copy(k_scales[1][:], kscale_pool[:].indirect(idx[:, entries[1]]))
+        gain = sb.tile([P, Q], F32, tag="q_bf", align_bytes=64)
+        nc.scalar.activation(gain[:], gain_pool[:].indirect(idx4[:]), COPY)
 
         a_sb = [sb.tile([P, I], F32, name=f"a_sb{h}") for h in range(Q_TILES)]
         for half in range(2):
@@ -118,10 +119,7 @@ def tile_attend_passedthrough_bymember_lean_pl_kernel(
                     a_ps[:], q_codes[h][:].bitcast(FP8X4), q_scales[h][:], k_words[half][:].bitcast(FP4X4),
                     k_scales[half][:], start=True, stop=True,
                 )
-                if h == 0:
-                    nc.vector.tensor_copy(a_sb[h][:, slots[half]], a_ps[:])
-                else:
-                    nc.scalar.copy(a_sb[h][:, slots[half]], a_ps[:])
+                nc.scalar.copy(a_sb[h][:, slots[half]], a_ps[:])
         for half in range(2):
             nc.vector.tensor_copy(f0[0][:].indirect(idx2[:, entries[half]]), a_sb[0][:, slots[half]])
             nc.scalar.activation(f0[1][:].indirect(idx2[:, entries[half]]), a_sb[1][:, slots[half]], COPY)
@@ -154,16 +152,16 @@ def tile_attend_passedthrough_bymember_lean_pl_kernel(
             )
         nc.vector.quantize_mx(w_codes[:].bitcast(FP8X4), w_scales[:], w_bf[:].rearrange("p q t -> p (q t)"))
 
-        v_listed = [
-            sb.tile([P, I], BF16, name=f"v_listed{j}", tag=("f0_0", "f0_1", "passed1", "passed0")[j], align_bytes=64)
-            for j in range(PACK)
-        ]
+        v_first = sb.tile([P, I], BF16, tag="f0_0", align_bytes=64)
+        v_odd = sb.tile([P, 2 * I], BF16, tag="f0_1", align_bytes=64)
+        v_third = sb.tile([P, I], BF16, tag="passed0", align_bytes=64)
+        v_listed = [v_first[:], v_odd[:, :I], v_third[:], v_odd[:, I:]]
         for j in range(PACK):
-            if j in (0, 3):
-                nc.vector.tensor_copy(v_listed[j][:], val_pool[j][:].indirect(idx[:]))
+            if j % 2 == 0:
+                nc.vector.tensor_copy(v_listed[j], val_pool[j][:].indirect(idx[:]))
             else:
-                nc.scalar.activation(v_listed[j][:], val_pool[j][:].indirect(idx[:]), COPY)
-        m_tags = ("passed0", "m1", "m2", "m3")
+                nc.scalar.activation(v_listed[j], val_pool[j][:].indirect(idx[:]), COPY)
+        m_tags = ("f0_1", "m1", "m2", "m3")
         m_listed = [None] * PACK
 
         def gather_member(j):
@@ -171,51 +169,61 @@ def tile_attend_passedthrough_bymember_lean_pl_kernel(
             nc.scalar.activation(m_listed[j][:], member_pool[j][:].indirect(idx4[:]), COPY)
 
         og = sb.tile([P, PACK, Q], F32)
-        for pair in range(2):
-            vt_ps = ps.tile([P, 2, 2, P], F32, tag=f"bank{4 * pair}")
-            for c in range(2):
-                words = v_listed[2 * pair + c][:].bitcast(F32)
+        groups = ((0, 1), (2, 3))
+        for n, planes in enumerate(groups):
+            width = len(planes)
+            vt_ps = ps.tile([P, width, 2, P], F32, tag=f"bank{(0, 4, 5)[n]}")
+            for c, j in enumerate(planes):
+                words = v_listed[j].bitcast(F32)
                 for u in range(2):
                     nc.tensor.transpose(vt_ps[:, c, u, :], words[:, u::2], ident[:])
             v_bf = sb.tile(
-                [P, 2 * P * PACK], BF16, align_bytes=64, name=f"v_bf{pair}", tag=("val_pool2", "v_bf1")[pair]
+                [P, width * P * PACK], BF16, align_bytes=64, name=f"v_bf{n}", tag="val_pool3" if n == 0 else f"v_bf{n}"
             )
             nc.scalar.copy(
-                v_bf[:].bitcast(F32).rearrange("p (c e u) -> p c e u", c=2, u=2),
+                v_bf[:].bitcast(F32).rearrange("p (c e u) -> p c e u", c=width, u=2),
                 vt_ps[:].rearrange("p c u e -> p c e u"),
             )
-            v_codes = sb.tile(
-                [P, 2 * P], U32, align_bytes=64, name=f"v_codes{pair}", tag=("val_pool3", "v_codes1")[pair]
-            )
-            v_scales = sb.tile([P, 2 * P], U8, align_bytes=64, name=f"v_scales{pair}")
+            v_codes = sb.tile([P, width * P], U32, align_bytes=64, name=f"v_codes{n}")
+            v_scales = sb.tile([P, width * P], U8, align_bytes=64, name=f"v_scales{n}")
             nc.vector.quantize_mx(v_codes[:].bitcast(FP8X4), v_scales[:], v_bf[:])
-            o_ps = ps.tile([P, 2, Q], F32, tag=f"bank{2 + pair}")
-            for c in range(2):
+            o_ps = ps.tile([P, width, Q], F32, tag=f"bank{(2, 3, 6)[n]}")
+            for c in range(width):
                 cols = slice(c * P, (c + 1) * P)
                 nc.tensor.matmul_mx(
                     o_ps[:, c, :], v_codes[:, cols].bitcast(FP8X4), v_scales[:, cols], w_codes[:].bitcast(FP8X4),
                     w_scales[:], start=True, stop=True,
                 )
             nc.vector.tensor_tensor(
-                og[:, 2 * pair : 2 * pair + 2, :], o_ps[:], gain[:].unsqueeze(1).to_broadcast([P, 2, Q]), ALU.mult
+                og[:, planes[0] : planes[0] + width, :], o_ps[:], gain[:].unsqueeze(1).to_broadcast([P, width, Q]),
+                ALU.mult,
             )
 
         y = sb.tile([P, PACK, Q], F32)
         for j in range(PACK):
             gather_member(j)
-        for j in range(PACK):
+        for j in range(PACK - 1):
             nc.vector.tensor_tensor(y[:, j, :], m_listed[j][:], og[:, j, :], ALU.add)
+        for h in range(Q_TILES):
+            cols = slice(h * P, (h + 1) * P)
+            nc.vector.tensor_tensor(y[:, PACK - 1, cols], m_listed[PACK - 1][:, cols], og[:, PACK - 1, cols], ALU.add)
         y_rows = out_0.rearrange("(p t) q -> p t q", t=PACK)
         nc.sync.dma_start(y_rows[:, : PACK - 1, :], y[:, : PACK - 1, :])
         nc.sync.dma_start(y_rows[:, PACK - 1, :], y[:, PACK - 1, :])
 
-        y_bf = sb.tile([P, Q, PACK], BF16, align_bytes=64)
-        nc.vector.tensor_copy(
-            y_bf[:].rearrange("p (c i) t -> p c t i", i=4), y[:].rearrange("p t (c i) -> p c t i", i=4)
-        )
+        y_bf = sb.tile([P, Q * PACK], BF16, align_bytes=64)
         y_codes = sb.tile([P, Q], U32, align_bytes=64)
         y_scales = sb.tile([P, Q], U8, align_bytes=64)
-        nc.vector.quantize_mx(y_codes[:].bitcast(FP8X4), y_scales[:], y_bf[:].rearrange("p q t -> p (q t)"))
+        for h in range(Q_TILES):
+            nc.vector.tensor_copy(
+                y_bf[:, h * P * PACK : (h + 1) * P * PACK].rearrange("p (c i t) -> p c t i", i=4, t=PACK),
+                y[:, :, h * P : (h + 1) * P].rearrange("p t (c i) -> p c t i", i=4),
+            )
+        for h in range(Q_TILES):
+            cols = slice(h * P, (h + 1) * P)
+            nc.vector.quantize_mx(
+                y_codes[:, cols].bitcast(FP8X4), y_scales[:, cols], y_bf[:, h * P * PACK : (h + 1) * P * PACK]
+            )
         nc.sync.dma_start(out_1[0].rearrange("p c r -> p (c r)").bitcast(I32), y_codes[:].bitcast(I32))
         for g in range(4):
             queue = nc.sync if g % 2 == 0 else nc.scalar

from contextlib import ExitStack

import concourse.mybir as mybir
from concourse.masks import make_identity

D, T, I, Q, E, Z, M = 512, 2048, 512, 256, 512, 1024, 1024
FLOPS = 2 * D * Q * I + 2 * I * E * Q
BYTES = 4 * (D * Q + I + E * T + E * M + M + E * Q) + D * T // 2 + D * T // 32 + 256 * (3 * I + Q) // 16 + E * Q + E * Q // 32

F32 = mybir.dt.float32
BF16 = mybir.dt.bfloat16
I32 = mybir.dt.int32
U32 = mybir.dt.uint32
U16 = mybir.dt.uint16
U8 = mybir.dt.uint8
FP8X4 = mybir.dt.float8_e4m3fn_x4
FP4X4 = mybir.dt.float4_e2m1fn_x4
ALU = mybir.AluOpType
COPY = mybir.ActivationFunctionType.Copy

P = 128
PACK = 4
Q_TILES = Q // P
HALF = I // 2


def tile_attend_passedthrough_bymember_lean_pl_kernel(
    tc, query, keys_words, keys_scales, slot_factor, vals, member, mgain, offs, offs2, offs3, offs4, out_0, out_1, out_2
):
    nc = tc.nc
    with ExitStack() as ctx:
        sb = ctx.enter_context(tc.tile_pool(name="sb", bufs=1))
        ps = ctx.enter_context(tc.psum_pool(name="ps", bufs=1))

        kscale_pool = sb.tile([P, T], U8, align_bytes=64)
        nc.gpsimd.memset(kscale_pool[:].bitcast(I32), 0)
        ident = sb.tile([P, P], F32)
        nc.vector.memset(ident[:], 0.0)
        make_identity(nc, ident[:], nomemset=True)
        f0 = [sb.tile([P, Z], F32, name=f"f0_{h}", tag=f"f0_{h}", align_bytes=64) for h in range(Q_TILES)]
        for h in range(Q_TILES):
            nc.vector.memset(f0[h][:], 0.0)

        gain_rows = sb.tile([P, M // P], F32, tag="q_bf", align_bytes=64)
        nc.scalar.dma_start(gain_rows[:], mgain[0:1, :].rearrange("o (p j) -> p (o j)", p=P))
        kword_pool = sb.tile([P, T], U16, align_bytes=64)
        nc.sync.dma_start(kword_pool[:].bitcast(I32), keys_words[0].bitcast(I32))
        idx = sb.tile([P, I // 16], U16)
        nc.sync.dma_start(idx[:], offs)
        q_raw = sb.tile([P, PACK, Q], F32, tag="q_raw", align_bytes=64)
        nc.sync.dma_start(q_raw[:], query.rearrange("(p t) q -> p t q", t=PACK))
        for g in range(4):
            nc.scalar.dma_start(
                kscale_pool[32 * g : 32 * g + 4, :].bitcast(I32), keys_scales[0, 4 * g : 4 * g + 4, :].bitcast(I32)
            )
        idx4 = sb.tile([P, Q // 16], U16)
        nc.sync.dma_start(idx4[:], offs4)
        idx2 = sb.tile([P, I // 16], U16)
        nc.sync.dma_start(idx2[:], offs2)
        vals_planes = vals.rearrange("(p j) t -> j p t", j=PACK)
        member_planes = member.rearrange("(p j) m -> j p m", j=PACK)
        val_pool = [
            sb.tile([P, T], F32, name=f"val_pool{j}", tag=f"val_pool{j}", align_bytes=64) for j in range(PACK)
        ]
        member_pool = [
            sb.tile([P, M], F32, name=f"member_pool{j}", tag=f"member_pool{j}", align_bytes=64) for j in range(PACK)
        ]
        nc.sync.dma_start(val_pool[0][:], vals_planes[0])
        idx3 = sb.tile([P, I // 16], U16)
        nc.sync.dma_start(idx3[:], offs3)
        os4 = sb.tile([P, PACK], F32)
        nc.sync.dma_start(os4[:], slot_factor.rearrange("o (p t) -> p (o t)", t=PACK))
        for j in range(1, PACK):
            nc.sync.dma_start(val_pool[j][:], vals_planes[j])
        for j in range(PACK):
            nc.sync.dma_start(member_pool[j][:], member_planes[j])

        gain_pool = sb.tile([P, M], F32, tag="gain_pool", align_bytes=64)
        for half in range(2):
            gain_ps = ps.tile([P, 4, P], F32, tag=f"bank{4 + half}")
            for c in range(4):
                j = 4 * half + c
                nc.tensor.transpose(gain_ps[:, c, :], gain_rows[:, j : j + 1].to_broadcast([P, P]), ident[:])
            nc.scalar.activation(
                gain_pool[:].rearrange("p (r j) -> p r j", j=M // P)[:, :, 4 * half : 4 * half + 4],
                gain_ps[:].rearrange("p c r -> p r c"),
                COPY,
            )

        slots = [slice(half * HALF, (half + 1) * HALF) for half in range(2)]
        entries = [slice(half * HALF // 16, (half + 1) * HALF // 16) for half in range(2)]
        k_words = [sb.tile([P, HALF], U16, align_bytes=64, name=f"k_words{half}") for half in range(2)]
        for half in range(2):
            nc.vector.tensor_copy(k_words[half][:], kword_pool[:].indirect(idx[:, entries[half]]))
        k_scales = [sb.tile([P, HALF], U8, align_bytes=64, name="k_scales0")]
        nc.vector.tensor_copy(k_scales[0][:], kscale_pool[:].indirect(idx[:, entries[0]]))
        q_codes = [sb.tile([P, P], U32, align_bytes=64, name=f"q_codes{h}") for h in range(Q_TILES)]
        q_scales = [sb.tile([P, P], U8, align_bytes=64, name=f"q_scales{h}") for h in range(Q_TILES)]
        q_bf = sb.tile([P, Q * PACK], BF16, align_bytes=64, tag="q_bf")
        for h in range(Q_TILES):
            q_tile = q_bf[:, h * P * PACK : (h + 1) * P * PACK]
            nc.scalar.activation(
                q_tile.rearrange("p (c i t) -> p c t i", i=4, t=PACK),
                q_raw[:, :, h * P : (h + 1) * P].rearrange("p t (c i) -> p c t i", i=4),
                COPY,
            )
            nc.vector.quantize_mx(q_codes[h][:].bitcast(FP8X4), q_scales[h][:], q_tile)

        k_scales.append(sb.tile([P, HALF], U8, align_bytes=64, name="k_scales1", tag="q_raw"))
        nc.vector.tensor_copy(k_scales[1][:], kscale_pool[:].indirect(idx[:, entries[1]]))
        gain = sb.tile([P, Q], F32, tag="q_bf", align_bytes=64)
        nc.scalar.activation(gain[:], gain_pool[:].indirect(idx4[:]), COPY)

        a_sb = [sb.tile([P, I], F32, name=f"a_sb{h}") for h in range(Q_TILES)]
        for half in range(2):
            for h in range(Q_TILES):
                a_ps = ps.tile([P, HALF], F32, tag=f"bank{2 * half + h}")
                nc.tensor.matmul_mx(
                    a_ps[:], q_codes[h][:].bitcast(FP8X4), q_scales[h][:], k_words[half][:].bitcast(FP4X4),
                    k_scales[half][:], start=True, stop=True,
                )
                nc.scalar.copy(a_sb[h][:, slots[half]], a_ps[:])
        for half in range(2):
            nc.vector.tensor_copy(f0[0][:].indirect(idx2[:, entries[half]]), a_sb[0][:, slots[half]])
            nc.scalar.activation(f0[1][:].indirect(idx2[:, entries[half]]), a_sb[1][:, slots[half]], COPY)

        passed = [sb.tile([P, I], F32, name=f"passed{h}", tag=f"passed{h}", align_bytes=64) for h in range(Q_TILES)]
        nc.vector.tensor_copy(passed[0][:], f0[0][:].indirect(idx3[:]))
        nc.scalar.activation(passed[1][:], f0[1][:].indirect(idx3[:]), COPY)
        st_ps = [ps.tile([P, PACK, P], F32, tag=f"bank{h}", name=f"st_ps{h}") for h in range(Q_TILES)]
        for h in range(Q_TILES):
            for t in range(PACK):
                nc.tensor.matmul(
                    st_ps[h][:, t, :], a_sb[h][:, t::PACK], ident[:], start=(t == 0), stop=False, is_transpose=True
                )
        w_bf = sb.tile([P, Q, PACK], BF16, align_bytes=64, tag="w_bf")
        w_codes = sb.tile([P, Q], U32, align_bytes=64)
        w_scales = sb.tile([P, Q], U8, align_bytes=64)
        for h in range(Q_TILES):
            for t in range(PACK):
                nc.tensor.matmul(
                    st_ps[h][:, t, :], passed[h][:, t::PACK], ident[:], start=False, stop=(t == PACK - 1),
                    is_transpose=True,
                )
            nc.vector.scalar_tensor_tensor(
                w_bf[:, h * P : (h + 1) * P, :],
                st_ps[h][:].rearrange("p t q -> p q t"),
                0.0,
                os4[:].unsqueeze(1).to_broadcast([P, P, PACK]),
                ALU.max,
                ALU.mult,
            )
        nc.vector.quantize_mx(w_codes[:].bitcast(FP8X4), w_scales[:], w_bf[:].rearrange("p q t -> p (q t)"))

        v_first = sb.tile([P, I], BF16, tag="f0_0", align_bytes=64)
        v_odd = sb.tile([P, 2 * I], BF16, tag="f0_1", align_bytes=64)
        v_third = sb.tile([P, I], BF16, tag="passed0", align_bytes=64)
        v_listed = [v_first[:], v_odd[:, :I], v_third[:], v_odd[:, I:]]
        for j in range(PACK):
            if j % 2 == 0:
                nc.vector.tensor_copy(v_listed[j], val_pool[j][:].indirect(idx[:]))
            else:
                nc.scalar.activation(v_listed[j], val_pool[j][:].indirect(idx[:]), COPY)
        m_tags = ("f0_1", "m1", "m2", "m3")
        m_listed = [None] * PACK

        def gather_member(j):
            m_listed[j] = sb.tile([P, Q], F32, name=f"m_listed{j}", tag=m_tags[j], align_bytes=64)
            nc.scalar.activation(m_listed[j][:], member_pool[j][:].indirect(idx4[:]), COPY)

        og = sb.tile([P, PACK, Q], F32)
        groups = ((0, 1), (2, 3))
        for n, planes in enumerate(groups):
            width = len(planes)
            vt_ps = ps.tile([P, width, 2, P], F32, tag=f"bank{(0, 4, 5)[n]}")
            for c, j in enumerate(planes):
                words = v_listed[j].bitcast(F32)
                for u in range(2):
                    nc.tensor.transpose(vt_ps[:, c, u, :], words[:, u::2], ident[:])
            v_bf = sb.tile(
                [P, width * P * PACK], BF16, align_bytes=64, name=f"v_bf{n}", tag="val_pool3" if n == 0 else f"v_bf{n}"
            )
            nc.scalar.copy(
                v_bf[:].bitcast(F32).rearrange("p (c e u) -> p c e u", c=width, u=2),
                vt_ps[:].rearrange("p c u e -> p c e u"),
            )
            v_codes = sb.tile([P, width * P], U32, align_bytes=64, name=f"v_codes{n}")
            v_scales = sb.tile([P, width * P], U8, align_bytes=64, name=f"v_scales{n}")
            nc.vector.quantize_mx(v_codes[:].bitcast(FP8X4), v_scales[:], v_bf[:])
            o_ps = ps.tile([P, width, Q], F32, tag=f"bank{(2, 3, 6)[n]}")
            for c in range(width):
                cols = slice(c * P, (c + 1) * P)
                nc.tensor.matmul_mx(
                    o_ps[:, c, :], v_codes[:, cols].bitcast(FP8X4), v_scales[:, cols], w_codes[:].bitcast(FP8X4),
                    w_scales[:], start=True, stop=True,
                )
            nc.vector.tensor_tensor(
                og[:, planes[0] : planes[0] + width, :], o_ps[:], gain[:].unsqueeze(1).to_broadcast([P, width, Q]),
                ALU.mult,
            )

        y = sb.tile([P, PACK, Q], F32)
        for j in range(PACK):
            gather_member(j)
        for j in range(PACK - 1):
            nc.vector.tensor_tensor(y[:, j, :], m_listed[j][:], og[:, j, :], ALU.add)
        for h in range(Q_TILES):
            cols = slice(h * P, (h + 1) * P)
            nc.vector.tensor_tensor(y[:, PACK - 1, cols], m_listed[PACK - 1][:, cols], og[:, PACK - 1, cols], ALU.add)
        y_rows = out_0.rearrange("(p t) q -> p t q", t=PACK)
        nc.sync.dma_start(y_rows[:, : PACK - 1, :], y[:, : PACK - 1, :])
        nc.sync.dma_start(y_rows[:, PACK - 1, :], y[:, PACK - 1, :])

        y_bf = sb.tile([P, Q * PACK], BF16, align_bytes=64)
        y_codes = sb.tile([P, Q], U32, align_bytes=64)
        y_scales = sb.tile([P, Q], U8, align_bytes=64)
        for h in range(Q_TILES):
            nc.vector.tensor_copy(
                y_bf[:, h * P * PACK : (h + 1) * P * PACK].rearrange("p (c i t) -> p c t i", i=4, t=PACK),
                y[:, :, h * P : (h + 1) * P].rearrange("p t (c i) -> p c t i", i=4),
            )
        for h in range(Q_TILES):
            cols = slice(h * P, (h + 1) * P)
            nc.vector.quantize_mx(
                y_codes[:, cols].bitcast(FP8X4), y_scales[:, cols], y_bf[:, h * P * PACK : (h + 1) * P * PACK]
            )
        nc.sync.dma_start(out_1[0].rearrange("p c r -> p (c r)").bitcast(I32), y_codes[:].bitcast(I32))
        for g in range(4):
            queue = nc.sync if g % 2 == 0 else nc.scalar
            queue.dma_start(
                out_2[0, 4 * g : 4 * g + 4, :].bitcast(I32), y_scales[32 * g : 32 * g + 4, :].bitcast(I32)
            )
